import numpy as np
import ml_dtypes


def mxq(x, axis, fmt="e4m3"):
    dtype, down = {"e4m3": (ml_dtypes.float8_e4m3fn, 7), "e5m2": (ml_dtypes.float8_e5m2, 14)}[fmt]
    v = np.moveaxis(np.asarray(x, np.float32).astype(ml_dtypes.bfloat16).astype(np.float64), axis, -1)
    blocks = v.reshape(v.shape[:-1] + (-1, 32))
    amax = np.abs(blocks).max(-1, keepdims=True)
    byte = np.maximum(np.where(amax > 0, np.frexp(amax)[1] - 1 + 127, 0) - down, 1)
    scale = np.exp2(byte - 127.0)
    codes = (blocks / scale).astype(np.float32).astype(dtype).astype(np.float64)
    return np.moveaxis((codes * scale).reshape(v.shape), -1, axis)


WIDE = False


def mx_kscale(k):
    if not WIDE:
        return np.ones(k)
    levels = np.array([10, -10, 5, -5, 0])
    if k % 512:
        return np.exp2(np.random.permutation(np.resize(levels, k // 32))).repeat(32)
    a = np.empty((k // 512, 16))
    for p in range(k // 512):
        a[p, :8] = np.random.permutation(np.resize(levels, 8))
        for g in range(8):
            far = levels[np.abs(levels - a[p, g]) >= 10]
            a[p, g + 8] = far[np.random.randint(len(far))]
    return np.exp2(a.ravel()).repeat(32)


def f64(x):
    return np.asarray(x).astype(np.float64)


def striped(idx):
    return np.tile(idx.reshape(-1, 16).T, (8, 1)).astype(np.uint16)


def unstriped(offs):
    return offs[:16].T.reshape(-1).astype(np.int64)


E2M1 = np.array([0.0, 0.5, 1.0, 1.5, 2.0, 3.0, 4.0, 6.0, -0.0, -0.5, -1.0, -1.5, -2.0, -3.0, -4.0, -6.0])


def pack_weight(w, fmt):
    k, n = w.shape
    w = f64(np.asarray(w, np.float32).astype(ml_dtypes.bfloat16)).reshape(k // 32, 32, n)
    amax = np.abs(w).max(1)
    if fmt == "e4m3":
        byte = np.frexp(amax)[1] - 1 + 127 - 7
    else:
        mant, ex = np.frexp(amax / 6.0)
        byte = np.where(mant > 0.5, ex, ex - 1) + 127
    byte = np.clip(np.where(amax > 0, byte, 1), 1, 254)
    scaled = (w * np.exp2(127.0 - byte)[:, None, :]).reshape(k, n).astype(np.float32)
    by_word = np.ascontiguousarray(scaled.reshape(k // 512, 128, 4, n).transpose(0, 1, 3, 2))
    if fmt == "e4m3":
        words = by_word.astype(ml_dtypes.float8_e4m3fn).view(np.uint8)
    else:
        c = by_word.astype(ml_dtypes.float4_e2m1fn).view(np.uint8) & 0xF
        words = (c[..., 0::2] | (c[..., 1::2] << 4)).reshape(k // 512, 128, 2 * n)
    return np.ascontiguousarray(words), np.ascontiguousarray(byte.astype(np.uint8).reshape(k // 512, 16, n))


def unpack_weight(words, scales, fmt):
    g, _, n = scales.shape
    words = np.ascontiguousarray(words).reshape(g, 128, n, -1)
    if fmt == "e4m3":
        vals = words.view(ml_dtypes.float8_e4m3fn).astype(np.float64)
    else:
        nib = np.empty((g, 128, n, 4), np.uint8)
        nib[..., 0::2] = words & 0xF
        nib[..., 1::2] = words >> 4
        vals = E2M1[nib]
    vals = vals * np.repeat(np.exp2(scales.astype(np.float64) - 127.0), 8, axis=1)[..., None]
    return vals.transpose(0, 1, 3, 2).reshape(g * 512, n)


def gelu(v):
    return 0.5 * v * (1.0 + np.tanh(np.sqrt(2.0 / np.pi) * (v + 0.044715 * v**3)))


def often(T, S):
    return np.random.permutation(T)[(T * np.random.uniform(0, 1, S) ** 4).astype(np.int64)]


K, K2, H, N, T, S, P = 1024, 512, 1024, 512, 4096, 1024, 512

def setup_inputs():
    n = np.random.standard_normal
    s, s2 = mx_kscale(K)[:, None], mx_kscale(K2)[:, None]
    u = mx_kscale(H)[:, None]
    d = {}
    d["tab_words"], d["tab_scales"] = pack_weight(n((K, T)) * s, "e4m3")
    d["tab2_words"], d["tab2_scales"] = pack_weight(n((K2, T)) * s2, "e4m3")
    d["tab3_words"], d["tab3_scales"] = pack_weight(n((K, T)) * s, "e4m3")
    d["w1"] = (n((K, H)) / s * u.T ** 2 * np.exp(0.7 * n((1, H))) / K ** 0.5).astype(np.float32)
    d["w2_words"], d["w2_scales"] = pack_weight(n((K2, H)) / s2 * u.T ** 2 * np.exp(0.7 * n((1, H))) / K2 ** 0.5, "e2m1")
    d["w3"] = (n((K, H)) / s * u.T / K ** 0.5).astype(np.float32)
    d["w4_words"], d["w4_scales"] = pack_weight(0.8 * n((H, N)) / u / H ** 0.5, "e4m3")
    d["target"] = n(N).astype(np.float32)
    d["offs"] = striped(np.random.permutation(T)[:S])
    d["offs2"] = striped(np.random.permutation(T)[:S])
    d["offs3"] = striped(np.random.permutation(T)[:S])
    d["pos1"] = striped(np.random.permutation(S)[:P])
    d["pos2"] = striped(often(S, P))
    d["pos3"] = striped(often(S, P))
    return d

def reference(tab_words, tab_scales, tab2_words, tab2_scales, tab3_words, tab3_scales, w1, w2_words, w2_scales,
              w3, w4_words, w4_scales, target, offs, offs2, offs3, pos1, pos2, pos3):
    v = unpack_weight(tab_words, tab_scales, "e4m3")[:, unstriped(offs)]
    v2 = unpack_weight(tab2_words, tab2_scales, "e4m3")[:, unstriped(offs2)]
    v3 = unpack_weight(tab3_words, tab3_scales, "e4m3")[:, unstriped(offs3)]
    a = mxq(f64(w1), 0, "e4m3").T @ v
    b = unpack_weight(w2_words, w2_scales, "e2m1").T @ v2
    d = mxq(f64(w3), 0, "e4m3").T @ v3
    z = np.sqrt(np.abs(a[:, unstriped(pos1)]) + np.abs(b[:, unstriped(pos2)])) - d[:, unstriped(pos3)]
    y = unpack_weight(w4_words, w4_scales, "e4m3").T @ mxq(z, 0, "e4m3")
    return np.square(y - f64(target)[:, None])

@@ -1,0 +1,265 @@
+from contextlib import ExitStack
+
+import concourse.mybir as mybir
+
+K, K2, H, N, T, S, J = 1024, 512, 1024, 512, 4096, 1024, 512
+FLOPS = 2 * (K * H * S + K2 * H * S + K * H * S + H * N * J)
+
+F32 = mybir.dt.float32
+BF16 = mybir.dt.bfloat16
+I32 = mybir.dt.int32
+U32 = mybir.dt.uint32
+U16 = mybir.dt.uint16
+U8 = mybir.dt.uint8
+FP8X4 = mybir.dt.float8_e4m3fn_x4
+FP4X4 = mybir.dt.float4_e2m1fn_x4
+ACT = mybir.ActivationFunctionType
+ALU = mybir.AluOpType
+
+P = 128
+PACK = 4
+K_PASS = P * PACK
+BANK = 512
+QUADS = 4
+
+
+def tile_list_bearing_target_miss_kernel(
+    tc, tab_words, tab_scales, tab2_words, tab2_scales, tab3_words, tab3_scales,
+    w1, w2_words, w2_scales, w3, w4_words, w4_scales, target,
+    offs, offs2, offs3, pos1, pos2, pos3, out,
+):
+    nc = tc.nc
+    with ExitStack() as ctx:
+        held = ctx.enter_context(tc.tile_pool(name="held", bufs=1))
+        ring = ctx.enter_context(tc.tile_pool(name="ring", bufs=1))
+        psum = ctx.enter_context(tc.psum_pool(name="psum", bufs=8))
+
+        def load_list(src, name):
+            t = held.tile(list(src.shape), U16, name=name)
+            nc.sync.dma_start(t[:], src)
+            return t
+
+        def zeroed_plane(width, name, engine):
+            t = held.tile([P, width], U8, name=name, align_bytes=64)
+            engine.memset(t[:].bitcast(I32), 0)
+            return t
+
+        def load_table_scales(plane, scales, queue):
+            passes = scales.shape[0]
+            for q in range(QUADS):
+                queue.dma_start(
+                    plane[32 * q : 32 * q + 4 * passes, :].bitcast(I32),
+                    scales[:, 4 * q : 4 * q + 4, :].bitcast(I32),
+                )
+
+        def load_table_words(words, a, name):
+            t = ring.tile([P, T], U32, name=name, tag="table", bufs=3)
+            nc.sync.dma_start(t[:].bitcast(I32), words[a].rearrange("p t i -> p (t i)").bitcast(I32))
+            return t
+
+        def load_weight(w, a, b, name):
+            t = ring.tile([P, PACK, K_PASS], F32, name=name, tag="wraw", bufs=4)
+            nc.sync.dma_start(
+                t[:],
+                w[a * K_PASS : (a + 1) * K_PASS, b * K_PASS : (b + 1) * K_PASS].rearrange("(p j) c -> p j c", j=PACK),
+            )
+            return t
+
+        def gather_bytes(window, offsets, dtype, name):
+            t = ring.tile([P, S], dtype, name=name, tag=name, bufs=1, align_bytes=64)
+            nc.vector.tensor_copy(t[:], window[:].indirect(offsets[:]))
+            return t
+
+        def round_weight(raw, a):
+            t = ring.tile([P, PACK * K_PASS], BF16, name="rounded", tag="rounded%d" % a, bufs=1, align_bytes=64)
+            nc.scalar.copy(
+                t[:].rearrange("p (t m j) -> p m j t", t=PACK, j=PACK),
+                raw[:].rearrange("p j (m t) -> p m j t", t=PACK),
+            )
+            return t
+
+        def quantise(rounded, name):
+            codes = held.tile([P, K_PASS], U32, name=name + "_codes", align_bytes=64)
+            plane = held.tile([P, K_PASS], U8, name=name + "_plane", align_bytes=64)
+            nc.vector.quantize_mx(out=codes[:].bitcast(FP8X4), scales=plane[:], in_=rounded[:])
+            return codes, plane
+
+        def first_stage(stationary, moving, func, name, lender=None):
+            if lender is None:
+                window = ring.tile([P, S], F32, name=name, tag="window", bufs=3, align_bytes=64)
+            else:
+                window = ring.tile([P, S], F32, name=name, tag=lender, bufs=1, align_bytes=64)
+            for h in range(S // BANK):
+                cols = slice(h * BANK, (h + 1) * BANK)
+                acc = psum.tile([P, BANK], F32, name="acc", tag="acc")
+                for a, ((lhs, lhs_scale), (words, plane)) in enumerate(zip(stationary, moving)):
+                    nc.tensor.matmul_mx(
+                        out=acc[:], lhsT=lhs, lhsT_scale=lhs_scale,
+                        rhs=words[:, cols].bitcast(FP8X4), rhs_scale=plane[4 * a : P, cols],
+                        start=(a == 0), stop=(a == len(moving) - 1),
+                    )
+                nc.scalar.activation(window[:, cols], acc[:], func)
+            return window
+
+        def quantised_columns(pieces, b, i):
+            cols = slice(i * P, (i + 1) * P)
+            return [(pieces[a, b][0][:, cols].bitcast(FP8X4), pieces[a, b][1][:, cols]) for a in range(2)]
+
+        row_tiles = [(b, i) for b in range(2) for i in range(PACK)]
+
+        tab2_plane = zeroed_plane(T, "tab2_plane", nc.vector)
+        w2_plane_raw = zeroed_plane(H, "w2_plane_raw", nc.vector)
+        tab_plane = zeroed_plane(T, "tab_plane", nc.vector)
+        tab3_plane = zeroed_plane(T, "tab3_plane", nc.vector)
+        w4_plane = zeroed_plane(2 * N, "w4_plane", nc.vector)
+
+        offs2_t = load_list(offs2, "offs2_t")
+        w2_raw = held.tile([P, 2 * H], U8, name="w2_raw")
+        nc.sync.dma_start(w2_raw[:].bitcast(I32), w2_words[0].bitcast(I32))
+        load_table_scales(tab2_plane, tab2_scales, nc.sync)
+        offs_t = load_list(offs, "offs_t")
+        tab2_win = load_table_words(tab2_words, 0, "tab2_win")
+        load_table_scales(w2_plane_raw, w2_scales, nc.sync)
+        pos2_t = load_list(pos2, "pos2_t")
+        load_table_scales(tab_plane, tab_scales, nc.sync)
+        w1_raw = {}
+        w1_raw[0, 0] = load_weight(w1, 0, 0, "w1_raw")
+        w1_raw[1, 0] = load_weight(w1, 1, 0, "w1_raw")
+        tab_win = [load_table_words(tab_words, a, "tab_win") for a in range(2)]
+        pos1_t = load_list(pos1, "pos1_t")
+        for a in range(2):
+            w1_raw[a, 1] = load_weight(w1, a, 1, "w1_raw")
+        offs3_t = load_list(offs3, "offs3_t")
+        load_table_scales(tab3_plane, tab3_scales, nc.sync)
+        pos3_t = load_list(pos3, "pos3_t")
+
+        w2_codes = held.tile([P, 2 * H], U8, name="w2_codes", align_bytes=64)
+        nc.vector.tensor_copy(
+            w2_codes[:].bitcast(U16).rearrange("p (b t m) -> p b m t", b=2, t=PACK),
+            w2_raw[:].bitcast(U16).rearrange("p (b m t) -> p b m t", b=2, t=PACK),
+        )
+        v2_plane = gather_bytes(tab2_plane, offs2_t, U8, "v2_plane")
+        v2_words = gather_bytes(tab2_win, offs2_t, U32, "v2_words")
+        w2_plane = held.tile([P, H], U8, name="w2_plane", align_bytes=64)
+        nc.vector.tensor_copy(
+            w2_plane[:].rearrange("p (b t m) -> p b t m", b=2, t=PACK),
+            w2_plane_raw[:].rearrange("p (b m t) -> p b t m", b=2, t=PACK),
+        )
+
+        v_plane = gather_bytes(tab_plane, offs_t, U8, "v_plane")
+        w1_q = {}
+        b_picked = {}
+        v_words = []
+        lenders = {0: "rounded0", 1: "rounded1", 3: "v_words0", 5: "v_words1", 6: "v3_plane"}
+        for n, (b, i) in enumerate(row_tiles):
+            c0 = b * K_PASS + i * P
+            lhs = (w2_codes[:, 2 * c0 : 2 * (c0 + P)].bitcast(FP4X4), w2_plane[:, c0 : c0 + P])
+            window = first_stage([lhs], [(v2_words, v2_plane)], ACT.Abs, "b_abs", lenders.get(n))
+            b_picked[b, i] = ring.tile([P, J], F32, name="b_picked", tag="part", bufs=10)
+            nc.vector.tensor_copy(b_picked[b, i][:], window[:].indirect(pos2_t[:]))
+            if n in (3, 5):
+                a = (n - 3) // 2
+                w1_q[a, 0] = quantise(round_weight(w1_raw[a, 0], a), "w1_%d0" % a)
+                v_words.append(gather_bytes(tab_win[a], offs_t, U32, "v_words%d" % a))
+
+        w3_raw = {}
+        for a in range(2):
+            w3_raw[a, 0] = load_weight(w3, a, 0, "w3_raw")
+        tab3_win = [load_table_words(tab3_words, a, "tab3_win") for a in range(2)]
+
+        v3_plane = gather_bytes(tab3_plane, offs3_t, U8, "v3_plane")
+        for a in range(2):
+            w1_q[a, 1] = quantise(round_weight(w1_raw[a, 1], a), "w1_%d1" % a)
+        for a in range(2):
+            w3_raw[a, 1] = load_weight(w3, a, 1, "w3_raw")
+        w4_codes = held.tile([P, 2, N], U32, name="w4_codes", align_bytes=64)
+        nc.sync.dma_start(w4_codes[:].bitcast(I32), w4_words.rearrange("a p c i -> p a (c i)").bitcast(I32))
+        for q in range(QUADS):
+            nc.sync.dma_start(
+                w4_plane[32 * q : 32 * q + 4, :].bitcast(I32).rearrange("r (a c) -> r a c", a=2),
+                w4_scales[:, 4 * q : 4 * q + 4, :].bitcast(I32).rearrange("a r c -> r a c"),
+            )
+        target_t = held.tile([P, N // P], F32, name="target_t")
+        with nc.allow_non_contiguous_dma(reason="one target value a partition and output tile"):
+            nc.sync.dma_start(target_t[:], target.rearrange("(c p) -> p c", p=P))
+
+        root = []
+        w3_q = {}
+        v3_words = []
+
+        def take_root(n):
+            nc.scalar.activation(root[n][:], root[n][:], ACT.Sqrt)
+
+        lenders = {3: "v3_words0", 4: "v3_words1"}
+        for n, (b, i) in enumerate(row_tiles):
+            window = first_stage(quantised_columns(w1_q, b, i), [(w, v_plane) for w in v_words], ACT.Abs, "a_abs", lenders.get(n))
+            root.append(ring.tile([P, J], F32, name="root", tag="part", bufs=10))
+            nc.vector.tensor_tensor(root[n][:], window[:].indirect(pos1_t[:]), b_picked[b, i][:], ALU.add)
+            if n in (2, 3):
+                a = n - 2
+                w3_q[a, 0] = quantise(round_weight(w3_raw[a, 0], a), "w3_%d0" % a)
+            if n in (3, 4):
+                a = n - 3
+                v3_words.append(gather_bytes(tab3_win[a], offs3_t, U32, "v3_words%d" % a))
+            if 2 <= n < 6:
+                take_root(n - 2)
+        for a in range(2):
+            w3_q[a, 1] = quantise(round_weight(w3_raw[a, 1], a), "w3_%d1" % a)
+
+        half = J // 2
+        halves = [slice(h * half, (h + 1) * half) for h in range(2)]
+        minus_z = [ring.tile([P, PACK, J], F32, name="minus_z", tag="minus_z", bufs=2) for b in range(2)]
+
+        def quantise_z(b, cols, engine, tag, name):
+            width = cols.stop - cols.start
+            rounded = ring.tile([P, PACK * width], BF16, name="rounded", tag=tag, bufs=1, align_bytes=64)
+            dst = rounded[:].rearrange("p (c e i) -> p c i e", e=4, i=PACK)
+            src = minus_z[b][:, :, cols].rearrange("p i (c e) -> p c i e", e=4)
+            if engine is nc.scalar:
+                nc.scalar.activation(dst, src, ACT.Copy, scale=-1.0)
+            else:
+                nc.vector.tensor_scalar(dst, src, -1.0, None, ALU.mult)
+            codes = held.tile([P, width], U32, name=name + "_codes", align_bytes=64)
+            plane = held.tile([P, width], U8, name=name + "_plane", align_bytes=64)
+            nc.vector.quantize_mx(out=codes[:].bitcast(FP8X4), scales=plane[:], in_=rounded[:])
+            return codes, plane
+
+        def d_window(b, i):
+            return first_stage(quantised_columns(w3_q, b, i), [(w, v3_plane) for w in v3_words], ACT.Copy, "d_win", d_lenders.get((b, i)))
+
+        d_lenders = {(1, 3): "v2_words"}
+        for i in range(PACK):
+            window = d_window(0, i)
+            nc.vector.tensor_tensor(minus_z[0][:, i, :], window[:].indirect(pos3_t[:]), root[i][:], ALU.subtract)
+        windows = []
+        for i in range(PACK):
+            take_root(PACK + i)
+            windows.append(d_window(1, i))
+        z0 = quantise_z(0, slice(0, J), nc.vector, "rounded0", "z0")
+
+        def pick(h, i):
+            offsets = pos3_t[:, h * half // 16 : (h + 1) * half // 16]
+            nc.vector.tensor_tensor(minus_z[1][:, i, halves[h]], windows[i][:].indirect(offsets), root[PACK + i][:, halves[h]], ALU.subtract)
+
+        def last_stage(h, z1):
+            for c in range(N // P):
+                cols = slice(c * P, (c + 1) * P)
+                acc = psum.tile([P, half], F32, name="acc", tag="acc")
+                moving = [(z0[0][:, halves[h]], z0[1][:, halves[h]]), (z1[0][:], z1[1][:])]
+                for a in range(2):
+                    nc.tensor.matmul_mx(
+                        out=acc[:], lhsT=w4_codes[:, a, cols].bitcast(FP8X4),
+                        lhsT_scale=w4_plane[:, a * N + c * P : a * N + (c + 1) * P],
+                        rhs=moving[a][0].bitcast(FP8X4), rhs_scale=moving[a][1],
+                        start=(a == 0), stop=(a == 1),
+                    )
+                miss = ring.tile([P, half], F32, name="miss", tag="miss", bufs=8)
+                nc.scalar.activation(miss[:], acc[:], ACT.Square, bias=target_t[:, c : c + 1], scale=-1.0)
+                nc.sync.dma_start(out[cols, halves[h]], miss[:])
+
+        for i in range(PACK):
+            pick(0, i)
+        last_stage(0, quantise_z(1, halves[0], nc.scalar, "rounded1", "z1_0"))
+        for i in range(PACK):
+            pick(1, i)
+        last_stage(1, quantise_z(1, halves[1], nc.vector, "rounded0", "z1_1"))

@@ -21,6 +21,16 @@ PACK = 4
 K_PASS = P * PACK
 BANK = 512
 QUADS = 4
+KIB = 1024
+
+REGION_KIB = [
+    ("table0", 16), ("table1", 16), ("table2", 16), ("table3", 16),
+    ("raw00", 8), ("raw10", 8), ("raw01", 24), ("raw11", 8),
+    ("minus_z0", 8), ("rounded0", 4), ("rounded1", 4),
+    ("tab_plane", 4), ("tab2_plane", 4), ("tab3_plane", 4),
+    ("v_words0", 4), ("v_words1", 4), ("v2_words", 4), ("v3_words0", 4), ("v3_words1", 4),
+]
+REGION_START = {name: KIB * sum(size for other, size in REGION_KIB[:n]) for n, (name, size) in enumerate(REGION_KIB)}
 
 
 def tile_list_bearing_target_miss_kernel(
@@ -31,64 +41,76 @@ def tile_list_bearing_target_miss_kernel(
     nc = tc.nc
     with ExitStack() as ctx:
         held = ctx.enter_context(tc.tile_pool(name="held", bufs=1))
-        ring = ctx.enter_context(tc.tile_pool(name="ring", bufs=1))
+        placed = ctx.enter_context(tc.tile_pool(name="placed", bufs=1))
+        ring = ctx.enter_context(tc.tile_pool(name="ring", bufs=3))
         psum = ctx.enter_context(tc.psum_pool(name="psum", bufs=8))
+
+        def place(shape, dtype, name, region, at_kib=0):
+            return placed.tile(shape, dtype, name=name, align_bytes=64, offset=REGION_START[region] + int(at_kib * KIB))
 
         def load_list(src, name):
             t = held.tile(list(src.shape), U16, name=name)
             nc.sync.dma_start(t[:], src)
             return t
 
-        def zeroed_plane(width, name, engine):
-            t = held.tile([P, width], U8, name=name, align_bytes=64)
-            engine.memset(t[:].bitcast(I32), 0)
+        def zeroed(t):
+            nc.vector.memset(t[:].bitcast(I32), 0)
             return t
 
-        def load_table_scales(plane, scales, queue):
+        def load_scale_rows(plane, scales, quads):
             passes = scales.shape[0]
-            for q in range(QUADS):
-                queue.dma_start(
+            for q in quads:
+                nc.sync.dma_start(
                     plane[32 * q : 32 * q + 4 * passes, :].bitcast(I32),
                     scales[:, 4 * q : 4 * q + 4, :].bitcast(I32),
                 )
 
-        def load_table_words(words, a, name):
-            t = ring.tile([P, T], U32, name=name, tag="table", bufs=3)
+        def load_table_words(words, a, name, region):
+            t = place([P, T], U32, name, region)
             nc.sync.dma_start(t[:].bitcast(I32), words[a].rearrange("p t i -> p (t i)").bitcast(I32))
             return t
 
         def load_weight(w, a, b, name):
-            t = ring.tile([P, PACK, K_PASS], F32, name=name, tag="wraw", bufs=4)
+            t = place([P, PACK, K_PASS], F32, "%s_raw%d%d" % (name, a, b), "raw%d%d" % (a, b), 2 if (a, b) == (0, 1) else 0)
             nc.sync.dma_start(
                 t[:],
                 w[a * K_PASS : (a + 1) * K_PASS, b * K_PASS : (b + 1) * K_PASS].rearrange("(p j) c -> p j c", j=PACK),
             )
             return t
 
-        def gather_bytes(window, offsets, dtype, name):
-            t = ring.tile([P, S], dtype, name=name, tag=name, bufs=1, align_bytes=64)
+        def gather_plane(window, offsets, name):
+            t = held.tile([P, S], U8, name=name, align_bytes=64)
             nc.vector.tensor_copy(t[:], window[:].indirect(offsets[:]))
             return t
 
-        def round_weight(raw, a):
-            t = ring.tile([P, PACK * K_PASS], BF16, name="rounded", tag="rounded%d" % a, bufs=1, align_bytes=64)
-            nc.scalar.copy(
+        def gather_words(window, offsets, name):
+            t = place([P, S], U32, name, name)
+            nc.vector.tensor_copy(t[:], window[:].indirect(offsets[:]))
+            return t
+
+        def round_weight(raw, name, where, copy):
+            t = place([P, PACK * K_PASS], BF16, name + "_rounded", *where)
+            copy(
                 t[:].rearrange("p (t m j) -> p m j t", t=PACK, j=PACK),
                 raw[:].rearrange("p j (m t) -> p m j t", t=PACK),
             )
             return t
 
-        def quantise(rounded, name):
-            codes = held.tile([P, K_PASS], U32, name=name + "_codes", align_bytes=64)
-            plane = held.tile([P, K_PASS], U8, name=name + "_plane", align_bytes=64)
+        def quantise(rounded, name, where=None):
+            width = rounded.shape[1] // PACK
+            if where is None:
+                codes = held.tile([P, width], U32, name=name + "_codes", align_bytes=64)
+            else:
+                codes = place([P, width], U32, name + "_codes", *where)
+            plane = held.tile([P, width], U8, name=name + "_plane", align_bytes=64)
             nc.vector.quantize_mx(out=codes[:].bitcast(FP8X4), scales=plane[:], in_=rounded[:])
             return codes, plane
 
-        def first_stage(stationary, moving, func, name, lender=None):
-            if lender is None:
-                window = ring.tile([P, S], F32, name=name, tag="window", bufs=3, align_bytes=64)
+        def first_stage(stationary, moving, func, name, where):
+            if where is None:
+                window = ring.tile([P, S], F32, name=name, tag="window")
             else:
-                window = ring.tile([P, S], F32, name=name, tag=lender, bufs=1, align_bytes=64)
+                window = place([P, S], F32, name, *where)
             for h in range(S // BANK):
                 cols = slice(h * BANK, (h + 1) * BANK)
                 acc = psum.tile([P, BANK], F32, name="acc", tag="acc")
@@ -105,73 +127,81 @@ def tile_list_bearing_target_miss_kernel(
             cols = slice(i * P, (i + 1) * P)
             return [(pieces[a, b][0][:, cols].bitcast(FP8X4), pieces[a, b][1][:, cols]) for a in range(2)]
 
+        def picked_tile(name, where):
+            if where is None:
+                return held.tile([P, J], F32, name=name)
+            return place([P, J], F32, name, *where)
+
         row_tiles = [(b, i) for b in range(2) for i in range(PACK)]
 
-        tab2_plane = zeroed_plane(T, "tab2_plane", nc.vector)
-        w2_plane_raw = zeroed_plane(H, "w2_plane_raw", nc.vector)
-        tab_plane = zeroed_plane(T, "tab_plane", nc.vector)
-        tab3_plane = zeroed_plane(T, "tab3_plane", nc.vector)
-        w4_plane = zeroed_plane(2 * N, "w4_plane", nc.vector)
+        tab2_plane = zeroed(place([P, T], U8, "tab2_plane", "tab2_plane"))
+        tab_plane = zeroed(place([P, T], U8, "tab_plane", "tab_plane"))
+        w2_plane_raw = zeroed(held.tile([P, H], U8, name="w2_plane_raw"))
+        tab3_plane = zeroed(place([P, T], U8, "tab3_plane", "tab3_plane"))
+        w4_plane = zeroed(held.tile([P, 2 * N], U8, name="w4_plane", align_bytes=64))
 
         offs2_t = load_list(offs2, "offs2_t")
         w2_raw = held.tile([P, 2 * H], U8, name="w2_raw")
         nc.sync.dma_start(w2_raw[:].bitcast(I32), w2_words[0].bitcast(I32))
-        load_table_scales(tab2_plane, tab2_scales, nc.sync)
+        load_scale_rows(tab2_plane, tab2_scales, range(QUADS))
         offs_t = load_list(offs, "offs_t")
-        tab2_win = load_table_words(tab2_words, 0, "tab2_win")
-        load_table_scales(w2_plane_raw, w2_scales, nc.sync)
-        pos2_t = load_list(pos2, "pos2_t")
-        load_table_scales(tab_plane, tab_scales, nc.sync)
         w1_raw = {}
-        w1_raw[0, 0] = load_weight(w1, 0, 0, "w1_raw")
-        w1_raw[1, 0] = load_weight(w1, 1, 0, "w1_raw")
-        tab_win = [load_table_words(tab_words, a, "tab_win") for a in range(2)]
-        pos1_t = load_list(pos1, "pos1_t")
-        for a in range(2):
-            w1_raw[a, 1] = load_weight(w1, a, 1, "w1_raw")
+        w1_raw[0, 0] = load_weight(w1, 0, 0, "w1")
+        load_scale_rows(tab_plane, tab_scales, range(QUADS))
         offs3_t = load_list(offs3, "offs3_t")
-        load_table_scales(tab3_plane, tab3_scales, nc.sync)
-        pos3_t = load_list(pos3, "pos3_t")
+        w1_raw[1, 0] = load_weight(w1, 1, 0, "w1")
+        load_scale_rows(w2_plane_raw, w2_scales, range(QUADS))
+        load_scale_rows(tab3_plane, tab3_scales, (0, 1))
+        tab2_win = load_table_words(tab2_words, 0, "tab2_win", "table0")
+        load_scale_rows(tab3_plane, tab3_scales, (2, 3))
+        pos2_t = load_list(pos2, "pos2_t")
+        for a in range(2):
+            w1_raw[a, 1] = load_weight(w1, a, 1, "w1")
+        tab_win = [load_table_words(tab_words, a, "tab_win%d" % a, "table%d" % (1 + a)) for a in range(2)]
+        pos1_t = load_list(pos1, "pos1_t")
 
         w2_codes = held.tile([P, 2 * H], U8, name="w2_codes", align_bytes=64)
         nc.vector.tensor_copy(
             w2_codes[:].bitcast(U16).rearrange("p (b t m) -> p b m t", b=2, t=PACK),
             w2_raw[:].bitcast(U16).rearrange("p (b m t) -> p b m t", b=2, t=PACK),
         )
-        v2_plane = gather_bytes(tab2_plane, offs2_t, U8, "v2_plane")
-        v2_words = gather_bytes(tab2_win, offs2_t, U32, "v2_words")
+
+        v2_plane = gather_plane(tab2_plane, offs2_t, "v2_plane")
+        v_plane = gather_plane(tab_plane, offs_t, "v_plane")
+        w1_q = {}
+        w1_q[0, 0] = quantise(round_weight(w1_raw[0, 0], "w1_00", ["rounded0"], nc.scalar.copy), "w1_00", ["tab_plane"])
         w2_plane = held.tile([P, H], U8, name="w2_plane", align_bytes=64)
         nc.vector.tensor_copy(
             w2_plane[:].rearrange("p (b t m) -> p b t m", b=2, t=PACK),
             w2_plane_raw[:].rearrange("p (b m t) -> p b t m", b=2, t=PACK),
         )
-
-        v_plane = gather_bytes(tab_plane, offs_t, U8, "v_plane")
-        w1_q = {}
-        b_picked = {}
+        w1_q[1, 0] = quantise(round_weight(w1_raw[1, 0], "w1_10", ["rounded1"], nc.scalar.copy), "w1_10", ["tab_plane", 2])
+        v2_words = gather_words(tab2_win, offs2_t, "v2_words")
+        v3_plane = gather_plane(tab3_plane, offs3_t, "v3_plane")
+        b_picked = []
         v_words = []
-        lenders = {0: "rounded0", 1: "rounded1", 3: "v_words0", 5: "v_words1", 6: "v3_plane"}
+        window_at = {1: ["rounded0"], 2: ["rounded1"], 3: ["v_words0"], 5: ["v_words1"]}
+        picked_at = {0: ["tab3_plane"], 1: ["tab3_plane", 2], 4: ["table1"], 5: ["table1", 2], 6: ["table2"], 7: ["table2", 2]}
         for n, (b, i) in enumerate(row_tiles):
             c0 = b * K_PASS + i * P
             lhs = (w2_codes[:, 2 * c0 : 2 * (c0 + P)].bitcast(FP4X4), w2_plane[:, c0 : c0 + P])
-            window = first_stage([lhs], [(v2_words, v2_plane)], ACT.Abs, "b_abs", lenders.get(n))
-            b_picked[b, i] = ring.tile([P, J], F32, name="b_picked", tag="part", bufs=10)
-            nc.vector.tensor_copy(b_picked[b, i][:], window[:].indirect(pos2_t[:]))
+            window = first_stage([lhs], [(v2_words, v2_plane)], ACT.Abs, "b_abs%d" % n, window_at.get(n))
+            b_picked.append(picked_tile("b_picked%d" % n, picked_at.get(n)))
+            nc.vector.tensor_copy(b_picked[n][:], window[:].indirect(pos2_t[:]))
             if n in (3, 5):
                 a = (n - 3) // 2
-                w1_q[a, 0] = quantise(round_weight(w1_raw[a, 0], a), "w1_%d0" % a)
-                v_words.append(gather_bytes(tab_win[a], offs_t, U32, "v_words%d" % a))
+                v_words.append(gather_words(tab_win[a], offs_t, "v_words%d" % a))
+        for a in range(2):
+            rounded = round_weight(w1_raw[a, 1], "w1_%d1" % a, ["rounded%d" % a], nc.scalar.copy)
+            w1_q[a, 1] = quantise(rounded, "w1_%d1" % a, ["table2", 4 + 2 * a])
 
         w3_raw = {}
         for a in range(2):
-            w3_raw[a, 0] = load_weight(w3, a, 0, "w3_raw")
-        tab3_win = [load_table_words(tab3_words, a, "tab3_win") for a in range(2)]
-
-        v3_plane = gather_bytes(tab3_plane, offs3_t, U8, "v3_plane")
+            w3_raw[a, 0] = load_weight(w3, a, 0, "w3")
+        tab3_win = [load_table_words(tab3_words, a, "tab3_win%d" % a, "table%d" % (3 * a)) for a in range(2)]
         for a in range(2):
-            w1_q[a, 1] = quantise(round_weight(w1_raw[a, 1], a), "w1_%d1" % a)
-        for a in range(2):
-            w3_raw[a, 1] = load_weight(w3, a, 1, "w3_raw")
+            w3_raw[a, 1] = load_weight(w3, a, 1, "w3")
+        pos3_t = load_list(pos3, "pos3_t")
         w4_codes = held.tile([P, 2, N], U32, name="w4_codes", align_bytes=64)
         nc.sync.dma_start(w4_codes[:].bitcast(I32), w4_words.rearrange("a p c i -> p a (c i)").bitcast(I32))
         for q in range(QUADS):
@@ -183,63 +213,73 @@ def tile_list_bearing_target_miss_kernel(
         with nc.allow_non_contiguous_dma(reason="one target value a partition and output tile"):
             nc.sync.dma_start(target_t[:], target.rearrange("(c p) -> p c", p=P))
 
-        root = []
+        total = []
         w3_q = {}
+        w3_rounded = {}
         v3_words = []
-
-        def take_root(n):
-            nc.scalar.activation(root[n][:], root[n][:], ACT.Sqrt)
-
-        lenders = {3: "v3_words0", 4: "v3_words1"}
+        window_at = {2: ["v3_words0"], 3: ["v3_words1"], 4: ["raw10"], 5: ["raw10", 4], 6: ["raw01"], 7: ["raw01", 4]}
+        total_at = {3: ["table0"], 4: ["table3"], 5: ["table3", 2], 6: ["table3", 4], 7: ["table3", 6]}
         for n, (b, i) in enumerate(row_tiles):
-            window = first_stage(quantised_columns(w1_q, b, i), [(w, v_plane) for w in v_words], ACT.Abs, "a_abs", lenders.get(n))
-            root.append(ring.tile([P, J], F32, name="root", tag="part", bufs=10))
-            nc.vector.tensor_tensor(root[n][:], window[:].indirect(pos1_t[:]), b_picked[b, i][:], ALU.add)
+            moving = [(w, v_plane) for w in v_words]
+            window = first_stage(quantised_columns(w1_q, b, i), moving, ACT.Abs, "a_abs%d" % n, window_at.get(n))
+            total.append(picked_tile("total%d" % n, total_at.get(n)))
+            nc.vector.tensor_tensor(total[n][:], window[:].indirect(pos1_t[:]), b_picked[n][:], ALU.add)
             if n in (2, 3):
                 a = n - 2
-                w3_q[a, 0] = quantise(round_weight(w3_raw[a, 0], a), "w3_%d0" % a)
-            if n in (3, 4):
-                a = n - 3
-                v3_words.append(gather_bytes(tab3_win[a], offs3_t, U32, "v3_words%d" % a))
-            if 2 <= n < 6:
-                take_root(n - 2)
+                v3_words.append(gather_words(tab3_win[a], offs3_t, "v3_words%d" % a))
+            if n == 3:
+                for a in range(2):
+                    rounded = round_weight(w3_raw[a, 0], "w3_%d0" % a, ["rounded%d" % a], nc.scalar.copy)
+                    w3_q[a, 0] = quantise(rounded, "w3_%d0" % a, ["table0", 2 + 2 * a])
+            if n == 5:
+                w3_rounded[0] = round_weight(w3_raw[0, 1], "w3_01", ["minus_z0"], nc.scalar.copy)
+        w3_rounded[1] = round_weight(w3_raw[1, 1], "w3_11", ["minus_z0", 4], nc.vector.tensor_copy)
         for a in range(2):
-            w3_q[a, 1] = quantise(round_weight(w3_raw[a, 1], a), "w3_%d1" % a)
+            w3_q[a, 1] = quantise(w3_rounded[a], "w3_%d1" % a)
+
+        roots = place([P, 2 * PACK, J], F32, "roots", "raw01", 8)
+
+        def take_root(n):
+            nc.scalar.activation(roots[:, n, :], total[n][:], ACT.Sqrt)
+
+        for n in range(6):
+            take_root(n)
 
         half = J // 2
         halves = [slice(h * half, (h + 1) * half) for h in range(2)]
-        minus_z = [ring.tile([P, PACK, J], F32, name="minus_z", tag="minus_z", bufs=2) for b in range(2)]
+        minus_z0 = place([P, PACK, J], F32, "minus_z0", "minus_z0")
+        minus_z1 = [place([P, PACK, half], F32, "minus_z1_%d" % h, "raw00", 4 * h) for h in range(2)]
 
-        def quantise_z(b, cols, engine, tag, name):
-            width = cols.stop - cols.start
-            rounded = ring.tile([P, PACK * width], BF16, name="rounded", tag=tag, bufs=1, align_bytes=64)
+        def round_z(minus_z, engine, region, name):
+            width = minus_z.shape[2]
+            rounded = place([P, PACK * width], BF16, name + "_rounded", region)
             dst = rounded[:].rearrange("p (c e i) -> p c i e", e=4, i=PACK)
-            src = minus_z[b][:, :, cols].rearrange("p i (c e) -> p c i e", e=4)
+            src = minus_z[:].rearrange("p i (c e) -> p c i e", e=4)
             if engine is nc.scalar:
                 nc.scalar.activation(dst, src, ACT.Copy, scale=-1.0)
             else:
                 nc.vector.tensor_scalar(dst, src, -1.0, None, ALU.mult)
-            codes = held.tile([P, width], U32, name=name + "_codes", align_bytes=64)
-            plane = held.tile([P, width], U8, name=name + "_plane", align_bytes=64)
-            nc.vector.quantize_mx(out=codes[:].bitcast(FP8X4), scales=plane[:], in_=rounded[:])
-            return codes, plane
+            return rounded
 
-        def d_window(b, i):
-            return first_stage(quantised_columns(w3_q, b, i), [(w, v3_plane) for w in v3_words], ACT.Copy, "d_win", d_lenders.get((b, i)))
+        window_at = {0: ["raw01"], 1: ["raw01", 4], 2: ["raw11"], 3: ["raw11", 4], 4: ["v_words0"], 5: ["v_words1"], 6: ["v2_words"]}
 
-        d_lenders = {(1, 3): "v2_words"}
+        def d_window(n):
+            moving = [(w, v3_plane) for w in v3_words]
+            return first_stage(quantised_columns(w3_q, *row_tiles[n]), moving, ACT.Copy, "d_win%d" % n, window_at.get(n))
+
         for i in range(PACK):
-            window = d_window(0, i)
-            nc.vector.tensor_tensor(minus_z[0][:, i, :], window[:].indirect(pos3_t[:]), root[i][:], ALU.subtract)
+            window = d_window(i)
+            nc.vector.tensor_tensor(minus_z0[:, i, :], window[:].indirect(pos3_t[:]), roots[:, i, :], ALU.subtract)
         windows = []
         for i in range(PACK):
-            take_root(PACK + i)
-            windows.append(d_window(1, i))
-        z0 = quantise_z(0, slice(0, J), nc.vector, "rounded0", "z0")
+            windows.append(d_window(PACK + i))
+            if i < 2:
+                take_root(6 + i)
+        z0 = quantise(round_z(minus_z0, nc.vector, "rounded0", "z0"), "z0")
 
         def pick(h, i):
             offsets = pos3_t[:, h * half // 16 : (h + 1) * half // 16]
-            nc.vector.tensor_tensor(minus_z[1][:, i, halves[h]], windows[i][:].indirect(offsets), root[PACK + i][:, halves[h]], ALU.subtract)
+            nc.vector.tensor_tensor(minus_z1[h][:, i, :], windows[i][:].indirect(offsets), roots[:, PACK + i, halves[h]], ALU.subtract)
 
         def last_stage(h, z1):
             for c in range(N // P):
@@ -253,13 +293,15 @@ def tile_list_bearing_target_miss_kernel(
                         rhs=moving[a][0].bitcast(FP8X4), rhs_scale=moving[a][1],
                         start=(a == 0), stop=(a == 1),
                     )
-                miss = ring.tile([P, half], F32, name="miss", tag="miss", bufs=8)
+                miss = held.tile([P, half], F32, name="miss%d%d" % (h, c))
                 nc.scalar.activation(miss[:], acc[:], ACT.Square, bias=target_t[:, c : c + 1], scale=-1.0)
                 nc.sync.dma_start(out[cols, halves[h]], miss[:])
 
         for i in range(PACK):
             pick(0, i)
-        last_stage(0, quantise_z(1, halves[0], nc.scalar, "rounded1", "z1_0"))
+        rounded = round_z(minus_z1[0], nc.scalar, "rounded1", "z1_0")
         for i in range(PACK):
             pick(1, i)
-        last_stage(1, quantise_z(1, halves[1], nc.vector, "rounded0", "z1_1"))
+            if i == 1:
+                last_stage(0, quantise(rounded, "z1_0", ["v_words1"]))
+        last_stage(1, quantise(round_z(minus_z1[1], nc.vector, "rounded0", "z1_1"), "z1_1"))

@@ -25,7 +25,7 @@ KIB = 1024
 
 REGION_KIB = [
     ("table0", 16), ("table1", 16), ("table2", 16), ("table3", 16),
-    ("raw00", 8), ("raw10", 8), ("raw01", 24), ("raw11", 8),
+    ("raw00", 8), ("raw10", 8), ("raw01", 16), ("raw11", 8),
     ("minus_z0", 8), ("rounded0", 4), ("rounded1", 4),
     ("tab_plane", 4), ("tab2_plane", 4), ("tab3_plane", 4),
     ("v_words0", 4), ("v_words1", 4), ("v2_words", 4), ("v3_words0", 4), ("v3_words1", 4),
@@ -65,6 +65,18 @@ def tile_list_bearing_target_miss_kernel(
                     scales[:, 4 * q : 4 * q + 4, :].bitcast(I32),
                 )
 
+        def load_spread_scale_rows(window, scales):
+            rows = scales.rearrange("a q t -> (a q) t").bitcast(I32)
+            nc.sync.dma_start(window[0:P:4, :].bitcast(I32), rows)
+
+        def carry_scale_rows(plane, picked, a):
+            for q in range(QUADS):
+                first = 4 * (16 * a + 4 * q)
+                nc.sync.dma_start(
+                    plane[32 * q + 4 * a : 32 * q + 4 * a + 4, :].bitcast(I32),
+                    picked[first : first + 16 : 4, :].bitcast(I32),
+                )
+
         def load_table_words(words, a, name, region):
             t = place([P, T], U32, name, region)
             nc.sync.dma_start(t[:].bitcast(I32), words[a].rearrange("p t i -> p (t i)").bitcast(I32))
@@ -88,11 +100,11 @@ def tile_list_bearing_target_miss_kernel(
             nc.vector.tensor_copy(t[:], window[:].indirect(offsets[:]))
             return t
 
-        def round_weight(raw, name, where, copy):
+        def round_weight(raw, name, where, copy, walk="p m j t"):
             t = place([P, PACK * K_PASS], BF16, name + "_rounded", *where)
             copy(
-                t[:].rearrange("p (t m j) -> p m j t", t=PACK, j=PACK),
-                raw[:].rearrange("p j (m t) -> p m j t", t=PACK),
+                t[:].rearrange("p (t m j) -> " + walk, t=PACK, j=PACK),
+                raw[:].rearrange("p j (m t) -> " + walk, t=PACK),
             )
             return t
 
@@ -138,6 +150,8 @@ def tile_list_bearing_target_miss_kernel(
         tab_plane = zeroed(place([P, T], U8, "tab_plane", "tab_plane"))
         w2_plane_raw = zeroed(held.tile([P, H], U8, name="w2_plane_raw"))
         tab3_plane = zeroed(place([P, T], U8, "tab3_plane", "tab3_plane"))
+        v_plane = zeroed(held.tile([P, S], U8, name="v_plane", align_bytes=64))
+        v3_plane = zeroed(held.tile([P, S], U8, name="v3_plane", align_bytes=64))
         w4_plane = zeroed(held.tile([P, 2 * N], U8, name="w4_plane", align_bytes=64))
 
         offs2_t = load_list(offs2, "offs2_t")
@@ -147,18 +161,15 @@ def tile_list_bearing_target_miss_kernel(
         offs_t = load_list(offs, "offs_t")
         w1_raw = {}
         w1_raw[0, 0] = load_weight(w1, 0, 0, "w1")
-        load_scale_rows(tab_plane, tab_scales, range(QUADS))
-        offs3_t = load_list(offs3, "offs3_t")
+        load_spread_scale_rows(tab_plane, tab_scales)
         w1_raw[1, 0] = load_weight(w1, 1, 0, "w1")
         load_scale_rows(w2_plane_raw, w2_scales, range(QUADS))
-        load_scale_rows(tab3_plane, tab3_scales, (0, 1))
         tab2_win = load_table_words(tab2_words, 0, "tab2_win", "table0")
-        load_scale_rows(tab3_plane, tab3_scales, (2, 3))
+        offs3_t = load_list(offs3, "offs3_t")
+        load_spread_scale_rows(tab3_plane, tab3_scales)
         pos2_t = load_list(pos2, "pos2_t")
         for a in range(2):
             w1_raw[a, 1] = load_weight(w1, a, 1, "w1")
-        tab_win = [load_table_words(tab_words, a, "tab_win%d" % a, "table%d" % (1 + a)) for a in range(2)]
-        pos1_t = load_list(pos1, "pos1_t")
 
         w2_codes = held.tile([P, 2 * H], U8, name="w2_codes", align_bytes=64)
         nc.vector.tensor_copy(
@@ -167,7 +178,7 @@ def tile_list_bearing_target_miss_kernel(
         )
 
         v2_plane = gather_plane(tab2_plane, offs2_t, "v2_plane")
-        v_plane = gather_plane(tab_plane, offs_t, "v_plane")
+        v_rows = gather_plane(tab_plane, offs_t, "v_rows")
         w1_q = {}
         w1_q[0, 0] = quantise(round_weight(w1_raw[0, 0], "w1_00", ["rounded0"], nc.scalar.copy), "w1_00", ["tab_plane"])
         w2_plane = held.tile([P, H], U8, name="w2_plane", align_bytes=64)
@@ -177,7 +188,12 @@ def tile_list_bearing_target_miss_kernel(
         )
         w1_q[1, 0] = quantise(round_weight(w1_raw[1, 0], "w1_10", ["rounded1"], nc.scalar.copy), "w1_10", ["tab_plane", 2])
         v2_words = gather_words(tab2_win, offs2_t, "v2_words")
-        v3_plane = gather_plane(tab3_plane, offs3_t, "v3_plane")
+        v3_rows = gather_plane(tab3_plane, offs3_t, "v3_rows")
+        tab_win = []
+        for a in range(2):
+            tab_win.append(load_table_words(tab_words, a, "tab_win%d" % a, "table%d" % (1 + a)))
+            carry_scale_rows(v_plane, v_rows, a)
+        pos1_t = load_list(pos1, "pos1_t")
         b_picked = []
         v_words = []
         window_at = {1: ["rounded0"], 2: ["rounded1"], 3: ["v_words0"], 5: ["v_words1"]}
@@ -198,7 +214,10 @@ def tile_list_bearing_target_miss_kernel(
         w3_raw = {}
         for a in range(2):
             w3_raw[a, 0] = load_weight(w3, a, 0, "w3")
-        tab3_win = [load_table_words(tab3_words, a, "tab3_win%d" % a, "table%d" % (3 * a)) for a in range(2)]
+        tab3_win = []
+        for a in range(2):
+            tab3_win.append(load_table_words(tab3_words, a, "tab3_win%d" % a, "table%d" % (3 * a)))
+            carry_scale_rows(v3_plane, v3_rows, a)
         for a in range(2):
             w3_raw[a, 1] = load_weight(w3, a, 1, "w3")
         pos3_t = load_list(pos3, "pos3_t")
@@ -232,27 +251,31 @@ def tile_list_bearing_target_miss_kernel(
                     rounded = round_weight(w3_raw[a, 0], "w3_%d0" % a, ["rounded%d" % a], nc.scalar.copy)
                     w3_q[a, 0] = quantise(rounded, "w3_%d0" % a, ["table0", 2 + 2 * a])
             if n == 5:
-                w3_rounded[0] = round_weight(w3_raw[0, 1], "w3_01", ["minus_z0"], nc.scalar.copy)
-        w3_rounded[1] = round_weight(w3_raw[1, 1], "w3_11", ["minus_z0", 4], nc.vector.tensor_copy)
+                w3_rounded[0] = round_weight(w3_raw[0, 1], "w3_01", ["table1", 10], nc.scalar.copy)
+        w3_rounded[1] = round_weight(w3_raw[1, 1], "w3_11", ["minus_z0", 4], nc.vector.tensor_copy, "p m t j")
         for a in range(2):
             w3_q[a, 1] = quantise(w3_rounded[a], "w3_%d1" % a)
 
-        roots = place([P, 2 * PACK, J], F32, "roots", "raw01", 8)
-
-        def take_root(n):
-            nc.scalar.activation(roots[:, n, :], total[n][:], ACT.Sqrt)
-
-        for n in range(6):
-            take_root(n)
-
         half = J // 2
         halves = [slice(h * half, (h + 1) * half) for h in range(2)]
-        minus_z0 = place([P, PACK, J], F32, "minus_z0", "minus_z0")
-        minus_z1 = [place([P, PACK, half], F32, "minus_z1_%d" % h, "raw00", 4 * h) for h in range(2)]
+        roots = place([P, PACK, J], F32, "roots", "raw01", 8)
 
-        def round_z(minus_z, engine, region, name):
+        late_roots = [place([P, PACK, half], F32, "late_roots%d" % h, "table1", 8 + 4 * h) for h in range(2)]
+
+        def take_late_root(i):
+            for h in range(2):
+                nc.scalar.activation(late_roots[h][:, i, :], total[PACK + i][:, halves[h]], ACT.Sqrt)
+
+        for i in range(PACK):
+            nc.scalar.activation(roots[:, i, :], total[i][:], ACT.Sqrt)
+        for i in range(2):
+            take_late_root(i)
+
+        minus_z0 = place([P, PACK, J], F32, "minus_z0", "minus_z0")
+
+        def round_z(minus_z, engine, where, name):
             width = minus_z.shape[2]
-            rounded = place([P, PACK * width], BF16, name + "_rounded", region)
+            rounded = place([P, PACK * width], BF16, name + "_rounded", *where)
             dst = rounded[:].rearrange("p (c e i) -> p c i e", e=4, i=PACK)
             src = minus_z[:].rearrange("p i (c e) -> p c i e", e=4)
             if engine is nc.scalar:
@@ -274,34 +297,46 @@ def tile_list_bearing_target_miss_kernel(
         for i in range(PACK):
             windows.append(d_window(PACK + i))
             if i < 2:
-                take_root(6 + i)
-        z0 = quantise(round_z(minus_z0, nc.vector, "rounded0", "z0"), "z0")
+                take_late_root(2 + i)
 
-        def pick(h, i):
-            offsets = pos3_t[:, h * half // 16 : (h + 1) * half // 16]
-            nc.vector.tensor_tensor(minus_z1[h][:, i, :], windows[i][:].indirect(offsets), roots[:, PACK + i, halves[h]], ALU.subtract)
+        def pick(cols, name, where):
+            width = cols.stop - cols.start
+            h = cols.start // half
+            minus_z = place([P, PACK, width], F32, name, *where)
+            offsets = pos3_t[:, cols.start // 16 : cols.stop // 16]
+            for i in range(PACK):
+                root = late_roots[h][:, i, cols.start - h * half : cols.stop - h * half]
+                nc.vector.tensor_tensor(minus_z[:, i, :], windows[i][:].indirect(offsets), root, ALU.subtract)
+            return minus_z
 
-        def last_stage(h, z1):
+        def last_stage(cols, z1):
+            width = cols.stop - cols.start
+            moving = [(z0[0][:, cols], z0[1][:, cols]), (z1[0][:], z1[1][:])]
             for c in range(N // P):
-                cols = slice(c * P, (c + 1) * P)
-                acc = psum.tile([P, half], F32, name="acc", tag="acc")
-                moving = [(z0[0][:, halves[h]], z0[1][:, halves[h]]), (z1[0][:], z1[1][:])]
+                rows = slice(c * P, (c + 1) * P)
+                acc = psum.tile([P, width], F32, name="acc", tag="acc")
                 for a in range(2):
                     nc.tensor.matmul_mx(
-                        out=acc[:], lhsT=w4_codes[:, a, cols].bitcast(FP8X4),
+                        out=acc[:], lhsT=w4_codes[:, a, rows].bitcast(FP8X4),
                         lhsT_scale=w4_plane[:, a * N + c * P : a * N + (c + 1) * P],
                         rhs=moving[a][0].bitcast(FP8X4), rhs_scale=moving[a][1],
                         start=(a == 0), stop=(a == 1),
                     )
-                miss = held.tile([P, half], F32, name="miss%d%d" % (h, c))
-                nc.scalar.activation(miss[:], acc[:], ACT.Square, bias=target_t[:, c : c + 1], scale=-1.0)
-                nc.sync.dma_start(out[cols, halves[h]], miss[:])
+                if c % 2 == 0:
+                    miss = held.tile([P, 2, width], F32, name="miss%d_%d" % (cols.start, c))
+                nc.scalar.activation(miss[:, c % 2, :], acc[:], ACT.Square, bias=target_t[:, c : c + 1], scale=-1.0)
+                if c % 2 == 1:
+                    pair = out[(c - 1) * P : (c + 1) * P, cols].rearrange("(c p) j -> p c j", p=P)
+                    nc.sync.dma_start(pair, miss[:])
 
-        for i in range(PACK):
-            pick(0, i)
-        rounded = round_z(minus_z1[0], nc.scalar, "rounded1", "z1_0")
-        for i in range(PACK):
-            pick(1, i)
-            if i == 1:
-                last_stage(0, quantise(rounded, "z1_0", ["v_words1"]))
-        last_stage(1, quantise(round_z(minus_z1[1], nc.vector, "rounded0", "z1_1"), "z1_1"))
+        pieces = [slice(0, 256), slice(256, 384), slice(384, 512)]
+        z0_rounded = round_z(minus_z0, nc.scalar, ["rounded0"], "z0")
+        first = pick(pieces[0], "minus_z1_0", ["raw00"])
+        first_rounded = round_z(first, nc.scalar, ["rounded1"], "z1_0")
+        second = pick(pieces[1], "minus_z1_1", ["table1", 8])
+        second_rounded = round_z(second, nc.scalar, ["rounded1", 2], "z1_1")
+        z0 = quantise(z0_rounded, "z0")
+        last_stage(pieces[0], quantise(first_rounded, "z1_0"))
+        third = pick(pieces[2], "minus_z1_2", ["rounded0", 3])
+        last_stage(pieces[1], quantise(second_rounded, "z1_1"))
+        last_stage(pieces[2], quantise(round_z(third, nc.vector, ["rounded1", 2], "z1_2"), "z1_2"))

from contextlib import ExitStack

import concourse.mybir as mybir

K, K2, H, N, T, S, J = 1024, 512, 1024, 512, 4096, 1024, 512
FLOPS = 2 * (K * H * S + K2 * H * S + K * H * S + H * N * J)

F32 = mybir.dt.float32
BF16 = mybir.dt.bfloat16
I32 = mybir.dt.int32
U32 = mybir.dt.uint32
U16 = mybir.dt.uint16
U8 = mybir.dt.uint8
FP8X4 = mybir.dt.float8_e4m3fn_x4
FP4X4 = mybir.dt.float4_e2m1fn_x4
ACT = mybir.ActivationFunctionType
ALU = mybir.AluOpType

P = 128
PACK = 4
K_PASS = P * PACK
BANK = 512
QUADS = 4
KIB = 1024

REGION_KIB = [
    ("table0", 16), ("table1", 16), ("table2", 16), ("table3", 16),
    ("raw00", 8), ("raw10", 8), ("raw01", 16), ("raw11", 8),
    ("minus_z0", 8), ("rounded0", 4), ("rounded1", 4),
    ("tab_plane", 4), ("tab2_plane", 4), ("tab3_plane", 4),
    ("v_words0", 4), ("v_words1", 4), ("v2_words", 4), ("v3_words0", 4), ("v3_words1", 4),
]
REGION_START = {name: KIB * sum(size for other, size in REGION_KIB[:n]) for n, (name, size) in enumerate(REGION_KIB)}


def tile_list_bearing_target_miss_kernel(
    tc, tab_words, tab_scales, tab2_words, tab2_scales, tab3_words, tab3_scales,
    w1, w2_words, w2_scales, w3, w4_words, w4_scales, target,
    offs, offs2, offs3, pos1, pos2, pos3, out,
):
    nc = tc.nc
    with ExitStack() as ctx:
        held = ctx.enter_context(tc.tile_pool(name="held", bufs=1))
        placed = ctx.enter_context(tc.tile_pool(name="placed", bufs=1))
        ring = ctx.enter_context(tc.tile_pool(name="ring", bufs=3))
        psum = ctx.enter_context(tc.psum_pool(name="psum", bufs=8))

        def place(shape, dtype, name, region, at_kib=0):
            return placed.tile(shape, dtype, name=name, align_bytes=64, offset=REGION_START[region] + int(at_kib * KIB))

        def load_list(src, name):
            t = held.tile(list(src.shape), U16, name=name)
            nc.sync.dma_start(t[:], src)
            return t

        def zeroed(t):
            nc.vector.memset(t[:].bitcast(I32), 0)
            return t

        def load_scale_rows(plane, scales, quads):
            passes = scales.shape[0]
            for q in quads:
                nc.sync.dma_start(
                    plane[32 * q : 32 * q + 4 * passes, :].bitcast(I32),
                    scales[:, 4 * q : 4 * q + 4, :].bitcast(I32),
                )

        def load_spread_scale_rows(window, scales):
            rows = scales.rearrange("a q t -> (a q) t").bitcast(I32)
            nc.sync.dma_start(window[0:P:4, :].bitcast(I32), rows)

        def carry_scale_rows(plane, picked, a):
            for q in range(QUADS):
                first = 4 * (16 * a + 4 * q)
                nc.sync.dma_start(
                    plane[32 * q + 4 * a : 32 * q + 4 * a + 4, :].bitcast(I32),
                    picked[first : first + 16 : 4, :].bitcast(I32),
                )

        def load_table_words(words, a, name, region):
            t = place([P, T], U32, name, region)
            nc.sync.dma_start(t[:].bitcast(I32), words[a].rearrange("p t i -> p (t i)").bitcast(I32))
            return t

        def load_weight(w, a, b, name):
            t = place([P, PACK, K_PASS], F32, "%s_raw%d%d" % (name, a, b), "raw%d%d" % (a, b), 2 if (a, b) == (0, 1) else 0)
            nc.sync.dma_start(
                t[:],
                w[a * K_PASS : (a + 1) * K_PASS, b * K_PASS : (b + 1) * K_PASS].rearrange("(p j) c -> p j c", j=PACK),
            )
            return t

        def gather_plane(window, offsets, name):
            t = held.tile([P, S], U8, name=name, align_bytes=64)
            nc.vector.tensor_copy(t[:], window[:].indirect(offsets[:]))
            return t

        def gather_words(window, offsets, name):
            t = place([P, S], U32, name, name)
            nc.vector.tensor_copy(t[:], window[:].indirect(offsets[:]))
            return t

        def round_weight(raw, name, where, copy, walk="p m j t"):
            t = place([P, PACK * K_PASS], BF16, name + "_rounded", *where)
            copy(
                t[:].rearrange("p (t m j) -> " + walk, t=PACK, j=PACK),
                raw[:].rearrange("p j (m t) -> " + walk, t=PACK),
            )
            return t

        def quantise(rounded, name, where=None):
            width = rounded.shape[1] // PACK
            if where is None:
                codes = held.tile([P, width], U32, name=name + "_codes", align_bytes=64)
            else:
                codes = place([P, width], U32, name + "_codes", *where)
            plane = held.tile([P, width], U8, name=name + "_plane", align_bytes=64)
            nc.vector.quantize_mx(out=codes[:].bitcast(FP8X4), scales=plane[:], in_=rounded[:])
            return codes, plane

        def first_stage(stationary, moving, func, name, where):
            if where is None:
                window = ring.tile([P, S], F32, name=name, tag="window")
            else:
                window = place([P, S], F32, name, *where)
            for h in range(S // BANK):
                cols = slice(h * BANK, (h + 1) * BANK)
                acc = psum.tile([P, BANK], F32, name="acc", tag="acc")
                for a, ((lhs, lhs_scale), (words, plane)) in enumerate(zip(stationary, moving)):
                    nc.tensor.matmul_mx(
                        out=acc[:], lhsT=lhs, lhsT_scale=lhs_scale,
                        rhs=words[:, cols].bitcast(FP8X4), rhs_scale=plane[4 * a : P, cols],
                        start=(a == 0), stop=(a == len(moving) - 1),
                    )
                nc.scalar.activation(window[:, cols], acc[:], func)
            return window

        def quantised_columns(pieces, b, i):
            cols = slice(i * P, (i + 1) * P)
            return [(pieces[a, b][0][:, cols].bitcast(FP8X4), pieces[a, b][1][:, cols]) for a in range(2)]

        def picked_tile(name, where):
            if where is None:
                return held.tile([P, J], F32, name=name)
            return place([P, J], F32, name, *where)

        row_tiles = [(b, i) for b in range(2) for i in range(PACK)]

        tab2_plane = zeroed(place([P, T], U8, "tab2_plane", "tab2_plane"))
        tab_plane = zeroed(place([P, T], U8, "tab_plane", "tab_plane"))
        w2_plane_raw = zeroed(held.tile([P, H], U8, name="w2_plane_raw"))
        tab3_plane = zeroed(place([P, T], U8, "tab3_plane", "tab3_plane"))
        v_plane = zeroed(held.tile([P, S], U8, name="v_plane", align_bytes=64))
        v3_plane = zeroed(held.tile([P, S], U8, name="v3_plane", align_bytes=64))
        w4_plane = zeroed(held.tile([P, 2 * N], U8, name="w4_plane", align_bytes=64))

        offs2_t = load_list(offs2, "offs2_t")
        w2_raw = held.tile([P, 2 * H], U8, name="w2_raw")
        nc.sync.dma_start(w2_raw[:].bitcast(I32), w2_words[0].bitcast(I32))
        load_scale_rows(tab2_plane, tab2_scales, range(QUADS))
        offs_t = load_list(offs, "offs_t")
        w1_raw = {}
        w1_raw[0, 0] = load_weight(w1, 0, 0, "w1")
        load_spread_scale_rows(tab_plane, tab_scales)
        w1_raw[1, 0] = load_weight(w1, 1, 0, "w1")
        load_scale_rows(w2_plane_raw, w2_scales, range(QUADS))
        tab2_win = load_table_words(tab2_words, 0, "tab2_win", "table0")
        offs3_t = load_list(offs3, "offs3_t")
        load_spread_scale_rows(tab3_plane, tab3_scales)
        pos2_t = load_list(pos2, "pos2_t")
        for a in range(2):
            w1_raw[a, 1] = load_weight(w1, a, 1, "w1")

        w2_codes = held.tile([P, 2 * H], U8, name="w2_codes", align_bytes=64)
        nc.vector.tensor_copy(
            w2_codes[:].bitcast(U16).rearrange("p (b t m) -> p b m t", b=2, t=PACK),
            w2_raw[:].bitcast(U16).rearrange("p (b m t) -> p b m t", b=2, t=PACK),
        )

        v2_plane = gather_plane(tab2_plane, offs2_t, "v2_plane")
        v_rows = gather_plane(tab_plane, offs_t, "v_rows")
        w1_q = {}
        w1_q[0, 0] = quantise(round_weight(w1_raw[0, 0], "w1_00", ["rounded0"], nc.scalar.copy), "w1_00", ["tab_plane"])
        w2_plane = held.tile([P, H], U8, name="w2_plane", align_bytes=64)
        nc.vector.tensor_copy(
            w2_plane[:].rearrange("p (b t m) -> p b t m", b=2, t=PACK),
            w2_plane_raw[:].rearrange("p (b m t) -> p b t m", b=2, t=PACK),
        )
        w1_q[1, 0] = quantise(round_weight(w1_raw[1, 0], "w1_10", ["rounded1"], nc.scalar.copy), "w1_10", ["tab_plane", 2])
        v2_words = gather_words(tab2_win, offs2_t, "v2_words")
        v3_rows = gather_plane(tab3_plane, offs3_t, "v3_rows")
        tab_win = []
        for a in range(2):
            tab_win.append(load_table_words(tab_words, a, "tab_win%d" % a, "table%d" % (1 + a)))
            carry_scale_rows(v_plane, v_rows, a)
        pos1_t = load_list(pos1, "pos1_t")
        b_picked = []
        v_words = []
        window_at = {1: ["rounded0"], 2: ["rounded1"], 3: ["v_words0"], 5: ["v_words1"]}
        picked_at = {0: ["tab3_plane"], 1: ["tab3_plane", 2], 4: ["table1"], 5: ["table1", 2], 6: ["table2"], 7: ["table2", 2]}
        for n, (b, i) in enumerate(row_tiles):
            c0 = b * K_PASS + i * P
            lhs = (w2_codes[:, 2 * c0 : 2 * (c0 + P)].bitcast(FP4X4), w2_plane[:, c0 : c0 + P])
            window = first_stage([lhs], [(v2_words, v2_plane)], ACT.Abs, "b_abs%d" % n, window_at.get(n))
            b_picked.append(picked_tile("b_picked%d" % n, picked_at.get(n)))
            nc.vector.tensor_copy(b_picked[n][:], window[:].indirect(pos2_t[:]))
            if n in (3, 5):
                a = (n - 3) // 2
                v_words.append(gather_words(tab_win[a], offs_t, "v_words%d" % a))
        for a in range(2):
            rounded = round_weight(w1_raw[a, 1], "w1_%d1" % a, ["rounded%d" % a], nc.scalar.copy)
            w1_q[a, 1] = quantise(rounded, "w1_%d1" % a, ["table2", 4 + 2 * a])

        w3_raw = {}
        for a in range(2):
            w3_raw[a, 0] = load_weight(w3, a, 0, "w3")
        tab3_win = []
        for a in range(2):
            tab3_win.append(load_table_words(tab3_words, a, "tab3_win%d" % a, "table%d" % (3 * a)))
            carry_scale_rows(v3_plane, v3_rows, a)
        for a in range(2):
            w3_raw[a, 1] = load_weight(w3, a, 1, "w3")
        pos3_t = load_list(pos3, "pos3_t")
        w4_codes = held.tile([P, 2, N], U32, name="w4_codes", align_bytes=64)
        nc.sync.dma_start(w4_codes[:].bitcast(I32), w4_words.rearrange("a p c i -> p a (c i)").bitcast(I32))
        for q in range(QUADS):
            nc.sync.dma_start(
                w4_plane[32 * q : 32 * q + 4, :].bitcast(I32).rearrange("r (a c) -> r a c", a=2),
                w4_scales[:, 4 * q : 4 * q + 4, :].bitcast(I32).rearrange("a r c -> r a c"),
            )
        target_t = held.tile([P, N // P], F32, name="target_t")
        with nc.allow_non_contiguous_dma(reason="one target value a partition and output tile"):
            nc.sync.dma_start(target_t[:], target.rearrange("(c p) -> p c", p=P))

        total = []
        w3_q = {}
        w3_rounded = {}
        v3_words = []
        window_at = {2: ["v3_words0"], 3: ["v3_words1"], 4: ["raw10"], 5: ["raw10", 4], 6: ["raw01"], 7: ["raw01", 4]}
        total_at = {3: ["table0"], 4: ["table3"], 5: ["table3", 2], 6: ["table3", 4], 7: ["table3", 6]}
        for n, (b, i) in enumerate(row_tiles):
            moving = [(w, v_plane) for w in v_words]
            window = first_stage(quantised_columns(w1_q, b, i), moving, ACT.Abs, "a_abs%d" % n, window_at.get(n))
            total.append(picked_tile("total%d" % n, total_at.get(n)))
            nc.vector.tensor_tensor(total[n][:], window[:].indirect(pos1_t[:]), b_picked[n][:], ALU.add)
            if n in (2, 3):
                a = n - 2
                v3_words.append(gather_words(tab3_win[a], offs3_t, "v3_words%d" % a))
            if n == 3:
                for a in range(2):
                    rounded = round_weight(w3_raw[a, 0], "w3_%d0" % a, ["rounded%d" % a], nc.scalar.copy)
                    w3_q[a, 0] = quantise(rounded, "w3_%d0" % a, ["table0", 2 + 2 * a])
            if n == 5:
                w3_rounded[0] = round_weight(w3_raw[0, 1], "w3_01", ["table1", 10], nc.scalar.copy)
        w3_rounded[1] = round_weight(w3_raw[1, 1], "w3_11", ["minus_z0", 4], nc.vector.tensor_copy, "p m t j")
        for a in range(2):
            w3_q[a, 1] = quantise(w3_rounded[a], "w3_%d1" % a)

        half = J // 2
        halves = [slice(h * half, (h + 1) * half) for h in range(2)]
        roots = place([P, PACK, J], F32, "roots", "raw01", 8)

        late_roots = [place([P, PACK, half], F32, "late_roots%d" % h, "table1", 8 + 4 * h) for h in range(2)]

        def take_late_root(i):
            for h in range(2):
                nc.scalar.activation(late_roots[h][:, i, :], total[PACK + i][:, halves[h]], ACT.Sqrt)

        for i in range(PACK):
            nc.scalar.activation(roots[:, i, :], total[i][:], ACT.Sqrt)
        for i in range(2):
            take_late_root(i)

        minus_z0 = place([P, PACK, J], F32, "minus_z0", "minus_z0")

        def round_z(minus_z, engine, where, name):
            width = minus_z.shape[2]
            rounded = place([P, PACK * width], BF16, name + "_rounded", *where)
            dst = rounded[:].rearrange("p (c e i) -> p c i e", e=4, i=PACK)
            src = minus_z[:].rearrange("p i (c e) -> p c i e", e=4)
            if engine is nc.scalar:
                nc.scalar.activation(dst, src, ACT.Copy, scale=-1.0)
            else:
                nc.vector.tensor_scalar(dst, src, -1.0, None, ALU.mult)
            return rounded

        window_at = {0: ["raw01"], 1: ["raw01", 4], 2: ["raw11"], 3: ["raw11", 4], 4: ["v_words0"], 5: ["v_words1"], 6: ["v2_words"]}

        def d_window(n):
            moving = [(w, v3_plane) for w in v3_words]
            return first_stage(quantised_columns(w3_q, *row_tiles[n]), moving, ACT.Copy, "d_win%d" % n, window_at.get(n))

        for i in range(PACK):
            window = d_window(i)
            nc.vector.tensor_tensor(minus_z0[:, i, :], window[:].indirect(pos3_t[:]), roots[:, i, :], ALU.subtract)
        windows = []
        for i in range(PACK):
            windows.append(d_window(PACK + i))
            if i < 2:
                take_late_root(2 + i)

        def pick(cols, name, where):
            width = cols.stop - cols.start
            h = cols.start // half
            minus_z = place([P, PACK, width], F32, name, *where)
            offsets = pos3_t[:, cols.start // 16 : cols.stop // 16]
            for i in range(PACK):
                root = late_roots[h][:, i, cols.start - h * half : cols.stop - h * half]
                nc.vector.tensor_tensor(minus_z[:, i, :], windows[i][:].indirect(offsets), root, ALU.subtract)
            return minus_z

        def last_stage(cols, z1):
            width = cols.stop - cols.start
            moving = [(z0[0][:, cols], z0[1][:, cols]), (z1[0][:], z1[1][:])]
            for c in range(N // P):
                rows = slice(c * P, (c + 1) * P)
                acc = psum.tile([P, width], F32, name="acc", tag="acc")
                for a in range(2):
                    nc.tensor.matmul_mx(
                        out=acc[:], lhsT=w4_codes[:, a, rows].bitcast(FP8X4),
                        lhsT_scale=w4_plane[:, a * N + c * P : a * N + (c + 1) * P],
                        rhs=moving[a][0].bitcast(FP8X4), rhs_scale=moving[a][1],
                        start=(a == 0), stop=(a == 1),
                    )
                if c % 2 == 0:
                    miss = held.tile([P, 2, width], F32, name="miss%d_%d" % (cols.start, c))
                nc.scalar.activation(miss[:, c % 2, :], acc[:], ACT.Square, bias=target_t[:, c : c + 1], scale=-1.0)
                if c % 2 == 1:
                    pair = out[(c - 1) * P : (c + 1) * P, cols].rearrange("(c p) j -> p c j", p=P)
                    nc.sync.dma_start(pair, miss[:])

        pieces = [slice(0, 256), slice(256, 384), slice(384, 512)]
        z0_rounded = round_z(minus_z0, nc.scalar, ["rounded0"], "z0")
        first = pick(pieces[0], "minus_z1_0", ["raw00"])
        first_rounded = round_z(first, nc.scalar, ["rounded1"], "z1_0")
        second = pick(pieces[1], "minus_z1_1", ["table1", 8])
        second_rounded = round_z(second, nc.scalar, ["rounded1", 2], "z1_1")
        z0 = quantise(z0_rounded, "z0")
        last_stage(pieces[0], quantise(first_rounded, "z1_0"))
        third = pick(pieces[2], "minus_z1_2", ["rounded0", 3])
        last_stage(pieces[1], quantise(second_rounded, "z1_1"))
        last_stage(pieces[2], quantise(round_z(third, nc.vector, ["rounded1", 2], "z1_2"), "z1_2"))
